import numpy as np
import ml_dtypes


def mxq(x, axis, fmt="e4m3"):
    dtype, down = {"e4m3": (ml_dtypes.float8_e4m3fn, 7), "e5m2": (ml_dtypes.float8_e5m2, 14)}[fmt]
    v = np.moveaxis(np.asarray(x, np.float32).astype(ml_dtypes.bfloat16).astype(np.float64), axis, -1)
    blocks = v.reshape(v.shape[:-1] + (-1, 32))
    amax = np.abs(blocks).max(-1, keepdims=True)
    byte = np.maximum(np.where(amax > 0, np.frexp(amax)[1] - 1 + 127, 0) - down, 1)
    scale = np.exp2(byte - 127.0)
    codes = (blocks / scale).astype(np.float32).astype(dtype).astype(np.float64)
    return np.moveaxis((codes * scale).reshape(v.shape), -1, axis)


WIDE = False


def mx_kscale(k):
    if not WIDE:
        return np.ones(k)
    levels = np.array([10, -10, 5, -5, 0])
    if k % 512:
        return np.exp2(np.random.permutation(np.resize(levels, k // 32))).repeat(32)
    a = np.empty((k // 512, 16))
    for p in range(k // 512):
        a[p, :8] = np.random.permutation(np.resize(levels, 8))
        for g in range(8):
            far = levels[np.abs(levels - a[p, g]) >= 10]
            a[p, g + 8] = far[np.random.randint(len(far))]
    return np.exp2(a.ravel()).repeat(32)


def f64(x):
    return np.asarray(x).astype(np.float64)


def striped(idx):
    return np.tile(idx.reshape(-1, 16).T, (8, 1)).astype(np.uint16)


def unstriped(offs):
    return offs[:16].T.reshape(-1).astype(np.int64)


K, T, S, V, N = 1024, 2048, 1024, 512, 256
P = 2 ** 7


def setup_inputs():
    n = np.random.standard_normal
    s = mx_kscale(K)[:, None]
    return {
        "xT": (n((K, T)) * s).astype(np.float32),
        "w1": (n((K, N)) / np.sqrt(K) / s).astype(np.float32),
        "fx": np.tile(np.random.uniform(0.05, 0.95, V), (P, 1)).astype(np.float32),
        "fy": np.tile(np.random.uniform(0.05, 0.95, V), (P, 1)).astype(np.float32),
        "offs": striped(np.random.permutation(T)[:S]),
        "c00": striped(np.random.permutation(S)[:V]),
        "c01": striped(np.random.permutation(S)[:V]),
        "c10": striped(np.random.permutation(S)[:V]),
        "c11": striped(np.random.permutation(S)[:V]),
    }


def reference(xT, w1, fx, fy, offs, c00, c01, c10, c11):
    xq = mxq(f64(xT)[:, unstriped(offs)], 0, "e4m3")
    y = mxq(f64(w1), 0, "e4m3").T @ xq
    top = y[:, unstriped(c00)] + (y[:, unstriped(c01)] - y[:, unstriped(c00)]) * f64(fx)[:1]
    low = y[:, unstriped(c10)] + (y[:, unstriped(c11)] - y[:, unstriped(c10)]) * f64(fx)[:1]
    return top + (low - top) * f64(fy)[:1]

@@ -1,0 +1,236 @@
+from contextlib import ExitStack
+
+import concourse.mybir as mybir
+from concourse.masks import make_identity
+
+K, T, S, V, N = 1024, 2048, 1024, 512, 256
+FLOPS = 2 * K * S * N
+
+F32 = mybir.dt.float32
+BF16 = mybir.dt.bfloat16
+U32 = mybir.dt.uint32
+I32 = mybir.dt.int32
+U16 = mybir.dt.uint16
+U8 = mybir.dt.uint8
+FP8X4 = mybir.dt.float8_e4m3fn_x4
+MULT = mybir.AluOpType.mult
+ADD = mybir.AluOpType.add
+
+P = 128
+PACK = 4
+K_PASS = P * PACK
+PASSES = K // K_PASS
+LANES = 16
+
+CHUNKS = [
+    [(0, 512, 0), (512, 1024, 0), (1024, 2048, 640)],
+    [(0, 1024, 0), (1024, 2048, 640)],
+    [(0, 1024, 0), (1024, 2048, 640)],
+    [(0, 1024, 256), (1024, 1536, 320), (1536, 2048, 320)],
+]
+
+
+def tile_picked_bilin_none_e_kernel(tc, xT, w1, fx, fy, offs, c00, c01, c10, c11, out):
+    nc = tc.nc
+    with ExitStack() as ctx:
+        keep = ctx.enter_context(tc.tile_pool(name="keep", bufs=1))
+        psum = ctx.enter_context(tc.psum_pool(name="psum", bufs=4))
+        psum_b = ctx.enter_context(tc.psum_pool(name="psum_b", bufs=2))
+
+        def bank(width):
+            return psum.tile([P, width], F32, name="bank")
+
+        def bank_b(width):
+            return psum_b.tile([P, width], F32, name="bank_b")
+
+        def load_list(src, name):
+            held = keep.tile([P, src.shape[1]], U16, name=name)
+            nc.sync.dma_start(held[:], src)
+            return held
+
+        def entries(held, a, b):
+            return held[:, a // LANES : b // LANES]
+
+        def load_chunk(q, c):
+            g, u = divmod(q, 2)
+            a, b = CHUNKS[q][c][:2]
+            raw = keep.tile([P, 2, b - a], F32, name="raw_%d_%d" % (q, c))
+            rows = xT[g * K_PASS : (g + 1) * K_PASS, a:b].rearrange("(p j) t -> p j t", j=PACK)
+            nc.sync.dma_start(out=raw[:], in_=rows[:, 2 * u : 2 * u + 2, :])
+            return raw
+
+        pairs = [keep.tile([P, T], U32, name="pairs_%d" % q) for q in range(2 * PASSES)]
+
+        def cast_chunk(q, c, raw):
+            a, b, on_vector = CHUNKS[q][c]
+            dst = pairs[q][:].bitcast(BF16).rearrange("p (t e) -> p t e", e=2)
+            src = raw[:].rearrange("p e t -> p t e")
+            cut = b - a - on_vector
+            nc.scalar.copy(out=dst[:, a : a + cut, :], in_=src[:, :cut, :])
+            if on_vector:
+                nc.vector.tensor_copy(out=dst[:, a + cut : b, :], in_=src[:, cut:, :])
+
+        picked = [keep.tile([P, 2, S], U32, name="picked_%d" % g) for g in range(PASSES)]
+        x_codes = [keep.tile([P, S], U32, name="x_codes_%d" % g, align_bytes=64) for g in range(PASSES)]
+        x_scales = [keep.tile([P, S], U8, name="x_scales_%d" % g, align_bytes=64) for g in range(PASSES)]
+        w_codes = [keep.tile([P, N], U32, name="w_codes_%d" % g, align_bytes=64) for g in range(PASSES)]
+        w_scales = [keep.tile([P, N], U8, name="w_scales_%d" % g, align_bytes=64) for g in range(PASSES)]
+
+        def gather(q, a, b):
+            g, u = divmod(q, 2)
+            nc.vector.tensor_copy(picked[g][:, u, a:b], pairs[q][:].indirect(entries(offs_sb, a, b)))
+
+        def weave(g, a, b, on_vector):
+            woven = keep.tile([P, 2 * (b - a)], U32, name="woven_%d_%d" % (g, a), align_bytes=64)
+            src = picked[g][:, :, a:b]
+            if on_vector:
+                nc.vector.tensor_copy(
+                    out=woven[:].bitcast(I32).rearrange("p (t u) -> p t u", u=2),
+                    in_=src.bitcast(I32).rearrange("p u t -> p t u"),
+                )
+            else:
+                nc.scalar.copy(out=woven[:].rearrange("p (t u) -> p t u", u=2), in_=src.rearrange("p u t -> p t u"))
+            return woven
+
+        def quantize(g, a, b, woven):
+            nc.vector.quantize_mx(
+                out=x_codes[g][:, a:b].bitcast(FP8X4), scales=x_scales[g][:, a:b], in_=woven[:].bitcast(BF16)
+            )
+
+        def multiply(acc, blk, g, a, b):
+            rows = slice(blk * P, (blk + 1) * P)
+            nc.tensor.matmul_mx(
+                out=acc[:],
+                lhsT=w_codes[g][:, rows].bitcast(FP8X4),
+                lhsT_scale=w_scales[g][:, rows],
+                rhs=x_codes[g][:, a:b].bitcast(FP8X4),
+                rhs_scale=x_scales[g][:, a:b],
+                start=(g == 0),
+                stop=(g == PASSES - 1),
+            )
+
+        raws = {}
+        raws[0, 0] = load_chunk(0, 0)
+        fx_sb = keep.tile([P, PACK], F32, name="fx_sb")
+        fy_sb = keep.tile([P, PACK], F32, name="fy_sb")
+        nc.sync.dma_start(out=fx_sb[:], in_=fx[0:1, :].rearrange("o (p c) -> (o p) c", c=PACK))
+        nc.sync.dma_start(out=fy_sb[:], in_=fy[0:1, :].rearrange("o (p c) -> (o p) c", c=PACK))
+        raws[0, 1] = load_chunk(0, 1)
+        offs_sb = load_list(offs, "offs_sb")
+        raws[0, 2] = load_chunk(0, 2)
+        for c in range(len(CHUNKS[1])):
+            raws[1, c] = load_chunk(1, c)
+        w_raw = []
+        for g in range(PASSES):
+            held = keep.tile([P, PACK, N], F32, name="w_raw_%d" % g)
+            nc.sync.dma_start(
+                out=held[:], in_=w1[g * K_PASS : (g + 1) * K_PASS, :].rearrange("(p j) m -> p j m", j=PACK)
+            )
+            w_raw.append(held)
+        for q in (2, 3):
+            for c in range(len(CHUNKS[q])):
+                raws[q, c] = load_chunk(q, c)
+        corners = [load_list(src, name) for src, name in ((c00, "c00_sb"), (c01, "c01_sb"), (c10, "c10_sb"), (c11, "c11_sb"))]
+
+        ident = keep.tile([P, P], F32, name="ident")
+        make_identity(nc, ident[:])
+        gx = keep.tile([P, PACK], F32, name="gx")
+        gy = keep.tile([P, PACK], F32, name="gy")
+        nc.vector.tensor_scalar(gx[:], fx_sb[:], -1.0, 1.0, MULT, ADD)
+        nc.vector.tensor_scalar(gy[:], fy_sb[:], -1.0, 1.0, MULT, ADD)
+        weights = []
+        for corner, (along_x, along_y) in enumerate(((gx, gy), (fx_sb, gy), (gx, fy_sb), (fx_sb, fy_sb))):
+            small = keep.tile([P, PACK], F32, name="small_%d" % corner)
+            nc.vector.tensor_tensor(small[:], along_x[:], along_y[:], MULT)
+            spread = bank(V)
+            for c in range(PACK):
+                nc.tensor.transpose(spread[:, c * P : (c + 1) * P], small[:, c : c + 1].to_broadcast([P, P]), ident[:])
+            wide = keep.tile([P, V], F32, name="wide_%d" % corner)
+            nc.vector.tensor_copy(
+                out=wide[:].rearrange("p (n c) -> p n c", c=PACK), in_=spread[:].rearrange("p (c n) -> p n c", c=PACK)
+            )
+            weights.append(wide)
+
+        for q in (0, 1):
+            for c in range(len(CHUNKS[q])):
+                cast_chunk(q, c, raws[q, c])
+            gather(q, 0, S)
+        HALF = S // 2
+        woven0 = [weave(0, a, a + HALF, True) for a in (0, HALF)]
+        for i, a in enumerate((0, HALF)):
+            quantize(0, a, a + HALF, woven0[i])
+        w_woven = []
+        for g in range(PASSES):
+            held = keep.tile([P, N, PACK], BF16, name="w_woven_%d" % g, align_bytes=64)
+            nc.vector.tensor_copy(out=held[:], in_=w_raw[g][:].rearrange("p j m -> p m j"))
+            w_woven.append(held)
+        for g in range(PASSES):
+            nc.vector.quantize_mx(
+                out=w_codes[g][:].bitcast(FP8X4), scales=w_scales[g][:], in_=w_woven[g][:].rearrange("p m j -> p (m j)")
+            )
+        QUARTER = S // 4
+        acc0 = [bank(QUARTER) for i in range(4)]
+        acc1 = [bank_b(HALF) for i in range(2)]
+        for i in range(4):
+            multiply(acc0[i], 0, 0, i * QUARTER, (i + 1) * QUARTER)
+        for i in range(2):
+            multiply(acc1[i], 1, 0, i * HALF, (i + 1) * HALF)
+
+        for c in range(len(CHUNKS[2])):
+            cast_chunk(2, c, raws[2, c])
+        gather(2, 0, S)
+        for c in range(len(CHUNKS[3])):
+            cast_chunk(3, c, raws[3, c])
+        y = [keep.tile([P, S], F32, name="y_%d" % blk) for blk in range(2)]
+        woven1 = []
+        for i in range(4):
+            gather(3, i * QUARTER, (i + 1) * QUARTER)
+            woven1.append(weave(1, i * QUARTER, (i + 1) * QUARTER, False))
+        for i in range(4):
+            quantize(1, i * QUARTER, (i + 1) * QUARTER, woven1[i])
+            multiply(acc0[i], 0, 1, i * QUARTER, (i + 1) * QUARTER)
+            nc.scalar.copy(out=y[0][:, i * QUARTER : (i + 1) * QUARTER], in_=acc0[i][:])
+        for i in range(2):
+            multiply(acc1[i], 1, 1, i * HALF, (i + 1) * HALF)
+            nc.scalar.copy(out=y[1][:, i * HALF : (i + 1) * HALF], in_=acc1[i][:])
+
+        def weighted(blk, corner, a, b):
+            prod = keep.tile([P, b - a], F32, name="prod_%d_%d_%d" % (blk, corner, a))
+            nc.vector.tensor_tensor(prod[:], y[blk][:].indirect(entries(corners[corner], a, b)), weights[corner][:, a:b], MULT)
+            return prod
+
+        def add_turned(sums, prod, a, b, first, last):
+            for s in range(a // P, b // P):
+                nc.tensor.matmul(
+                    sums[s][:], prod[:, s * P - a : (s + 1) * P - a], ident[:], start=first, stop=last, is_transpose=True
+                )
+
+        def turn_back(blk, sums, a, b):
+            back = bank_b(b - a)
+            for s in range(a // P, b // P):
+                turned = keep.tile([P, P], F32, name="turned_%d_%d" % (blk, s))
+                nc.scalar.copy(out=turned[:], in_=sums[s][:])
+                nc.tensor.transpose(back[:, s * P - a : (s + 1) * P - a], turned[:], ident[:])
+            return back
+
+        sums = [bank(P) for s in range(V // P)]
+        for corner in range(4):
+            add_turned(sums, weighted(0, corner, 0, V), 0, V, corner == 0, corner == 3)
+        back = turn_back(0, sums, 0, V)
+        result = keep.tile([P, V], F32, name="result_0")
+        nc.scalar.copy(out=result[:], in_=back[:])
+        nc.sync.dma_start(out=out[0:P, :], in_=result[:])
+
+        HV = V // 2
+        sums = [bank(P) for s in range(V // P)]
+        for corner in range(2):
+            add_turned(sums, weighted(1, corner, 0, V), 0, V, corner == 0, False)
+        backs = []
+        for a in (0, HV):
+            add_turned(sums, weighted(1, 2, a, a + HV), a, a + HV, False, True)
+            backs.append(turn_back(1, sums, a, a + HV))
+        lasts = [weighted(1, 3, a, a + HV) for a in (0, HV)]
+        for i, a in enumerate((0, HV)):
+            result = keep.tile([P, HV], F32, name="result_1_%d" % i)
+            nc.vector.tensor_tensor(result[:], backs[i][:], lasts[i][:], ADD)
+            nc.sync.dma_start(out=out[P : 2 * P, a : a + HV], in_=result[:])

@@ -23,10 +23,10 @@ PASSES = K // K_PASS
 LANES = 16
 
 CHUNKS = [
-    [(0, 512, 0), (512, 1024, 0), (1024, 2048, 640)],
-    [(0, 1024, 0), (1024, 2048, 640)],
-    [(0, 1024, 0), (1024, 2048, 640)],
-    [(0, 1024, 256), (1024, 1536, 320), (1536, 2048, 320)],
+    [(1280, 2048, 0), (640, 1280, 0), (0, 640, 0)],
+    [(1024, 2048, 0), (0, 1024, 640)],
+    [(1280, 2048, 0), (640, 1280, 0), (0, 640, 0)],
+    [(1024, 2048, 0), (512, 1024, 512), (0, 512, 336)],
 ]
 
 
@@ -54,55 +54,59 @@ def tile_picked_bilin_none_e_kernel(tc, xT, w1, fx, fy, offs, c00, c01, c10, c11
         def load_chunk(q, c):
             g, u = divmod(q, 2)
             a, b = CHUNKS[q][c][:2]
-            raw = keep.tile([P, 2, b - a], F32, name="raw_%d_%d" % (q, c))
+            raw = keep.tile([P, 2, b - a], F32, name="raw_%d_%d" % (q, c), align_bytes=64)
             rows = xT[g * K_PASS : (g + 1) * K_PASS, a:b].rearrange("(p j) t -> p j t", j=PACK)
             nc.sync.dma_start(out=raw[:], in_=rows[:, 2 * u : 2 * u + 2, :])
             return raw
 
-        pairs = [keep.tile([P, T], U32, name="pairs_%d" % q) for q in range(2 * PASSES)]
+        pair_tiles = [keep.tile([P, T], U32, name="pairs_%d" % q) for q in range(2 * PASSES)]
+        pairs = [held[:] for held in pair_tiles]
 
         def cast_chunk(q, c, raw):
             a, b, on_vector = CHUNKS[q][c]
-            dst = pairs[q][:].bitcast(BF16).rearrange("p (t e) -> p t e", e=2)
+            dst = pairs[q].bitcast(BF16).rearrange("p (t e) -> p t e", e=2)
             src = raw[:].rearrange("p e t -> p t e")
-            cut = b - a - on_vector
-            nc.scalar.copy(out=dst[:, a : a + cut, :], in_=src[:, :cut, :])
+            if on_vector < b - a:
+                nc.scalar.copy(out=dst[:, a + on_vector : b, :], in_=src[:, on_vector:, :])
             if on_vector:
-                nc.vector.tensor_copy(out=dst[:, a + cut : b, :], in_=src[:, cut:, :])
+                nc.vector.tensor_copy(out=dst[:, a : a + on_vector, :], in_=src[:, :on_vector, :])
 
-        picked = [keep.tile([P, 2, S], U32, name="picked_%d" % g) for g in range(PASSES)]
+        picked = [keep.tile([P, 2 * S], U32, name="picked_%d" % g, align_bytes=64) for g in range(PASSES)]
         x_codes = [keep.tile([P, S], U32, name="x_codes_%d" % g, align_bytes=64) for g in range(PASSES)]
         x_scales = [keep.tile([P, S], U8, name="x_scales_%d" % g, align_bytes=64) for g in range(PASSES)]
-        w_codes = [keep.tile([P, N], U32, name="w_codes_%d" % g, align_bytes=64) for g in range(PASSES)]
-        w_scales = [keep.tile([P, N], U8, name="w_scales_%d" % g, align_bytes=64) for g in range(PASSES)]
+        w_codes = [keep.tile([P, PASSES * P], U32, name="w_codes_%d" % blk, align_bytes=64) for blk in range(2)]
+        w_scales = [keep.tile([P, PASSES * P], U8, name="w_scales_%d" % blk, align_bytes=64) for blk in range(2)]
 
         def gather(q, a, b):
             g, u = divmod(q, 2)
-            nc.vector.tensor_copy(picked[g][:, u, a:b], pairs[q][:].indirect(entries(offs_sb, a, b)))
+            nc.vector.tensor_copy(picked[g][:, u * S + a : u * S + b], pairs[q].indirect(entries(offs_sb, a, b)))
 
-        def weave(g, a, b, on_vector):
+        def own_woven(g, a, b):
             woven = keep.tile([P, 2 * (b - a)], U32, name="woven_%d_%d" % (g, a), align_bytes=64)
-            src = picked[g][:, :, a:b]
+            return woven[:]
+
+        def weave(g, a, b, on_vector, woven):
+            src = picked[g][:].rearrange("p (u t) -> p u t", u=2)[:, :, a:b]
             if on_vector:
                 nc.vector.tensor_copy(
-                    out=woven[:].bitcast(I32).rearrange("p (t u) -> p t u", u=2),
+                    out=woven.bitcast(I32).rearrange("p (t u) -> p t u", u=2),
                     in_=src.bitcast(I32).rearrange("p u t -> p t u"),
                 )
             else:
-                nc.scalar.copy(out=woven[:].rearrange("p (t u) -> p t u", u=2), in_=src.rearrange("p u t -> p t u"))
+                nc.scalar.copy(out=woven.rearrange("p (t u) -> p t u", u=2), in_=src.rearrange("p u t -> p t u"))
             return woven
 
         def quantize(g, a, b, woven):
             nc.vector.quantize_mx(
-                out=x_codes[g][:, a:b].bitcast(FP8X4), scales=x_scales[g][:, a:b], in_=woven[:].bitcast(BF16)
+                out=x_codes[g][:, a:b].bitcast(FP8X4), scales=x_scales[g][:, a:b], in_=woven.bitcast(BF16)
             )
 
         def multiply(acc, blk, g, a, b):
-            rows = slice(blk * P, (blk + 1) * P)
+            rows = slice(g * P, (g + 1) * P)
             nc.tensor.matmul_mx(
                 out=acc[:],
-                lhsT=w_codes[g][:, rows].bitcast(FP8X4),
-                lhsT_scale=w_scales[g][:, rows],
+                lhsT=w_codes[blk][:, rows].bitcast(FP8X4),
+                lhsT_scale=w_scales[blk][:, rows],
                 rhs=x_codes[g][:, a:b].bitcast(FP8X4),
                 rhs_scale=x_scales[g][:, a:b],
                 start=(g == 0),
@@ -110,27 +114,47 @@ def tile_picked_bilin_none_e_kernel(tc, xT, w1, fx, fy, offs, c00, c01, c10, c11
             )
 
         raws = {}
-        raws[0, 0] = load_chunk(0, 0)
         fx_sb = keep.tile([P, PACK], F32, name="fx_sb")
         fy_sb = keep.tile([P, PACK], F32, name="fy_sb")
         nc.sync.dma_start(out=fx_sb[:], in_=fx[0:1, :].rearrange("o (p c) -> (o p) c", c=PACK))
         nc.sync.dma_start(out=fy_sb[:], in_=fy[0:1, :].rearrange("o (p c) -> (o p) c", c=PACK))
+        raws[0, 0] = load_chunk(0, 0)
         raws[0, 1] = load_chunk(0, 1)
         offs_sb = load_list(offs, "offs_sb")
         raws[0, 2] = load_chunk(0, 2)
         for c in range(len(CHUNKS[1])):
             raws[1, c] = load_chunk(1, c)
-        w_raw = []
-        for g in range(PASSES):
-            held = keep.tile([P, PACK, N], F32, name="w_raw_%d" % g)
-            nc.sync.dma_start(
-                out=held[:], in_=w1[g * K_PASS : (g + 1) * K_PASS, :].rearrange("(p j) m -> p j m", j=PACK)
-            )
-            w_raw.append(held)
         for q in (2, 3):
             for c in range(len(CHUNKS[q])):
                 raws[q, c] = load_chunk(q, c)
+
+        def load_w(blk, g):
+            held = keep.tile([P, PACK, P], F32, name="w_raw_%d_%d" % (blk, g), align_bytes=64)
+            rows = w1[g * K_PASS : (g + 1) * K_PASS, blk * P : (blk + 1) * P]
+            nc.sync.dma_start(out=held[:], in_=rows.rearrange("(p j) m -> p j m", j=PACK))
+            return held
+
+        w_raw = {(0, g): load_w(0, g) for g in range(PASSES)}
         corners = [load_list(src, name) for src, name in ((c00, "c00_sb"), (c01, "c01_sb"), (c10, "c10_sb"), (c11, "c11_sb"))]
+        for g in range(PASSES):
+            w_raw[1, g] = load_w(1, g)
+
+        def own_w(blk, g, tag):
+            held = keep.tile([P, P * PACK], BF16, name="w_woven_%d_%d" % (blk, g), tag=tag, align_bytes=64)
+            return held[:]
+
+        def weave_w(blk, g, held):
+            dst = held.rearrange("p (m j) -> p m j", j=PACK)
+            src = w_raw[blk, g][:].rearrange("p j m -> p m j")
+            if blk == 0:
+                nc.scalar.copy(out=dst, in_=src)
+            else:
+                nc.vector.tensor_copy(out=dst, in_=src)
+            return held
+
+        def quantize_w(blk, g, held):
+            rows = slice(g * P, (g + 1) * P)
+            nc.vector.quantize_mx(out=w_codes[blk][:, rows].bitcast(FP8X4), scales=w_scales[blk][:, rows], in_=held)
 
         ident = keep.tile([P, P], F32, name="ident")
         make_identity(nc, ident[:])
@@ -156,25 +180,10 @@ def tile_picked_bilin_none_e_kernel(tc, xT, w1, fx, fy, offs, c00, c01, c10, c11
                 cast_chunk(q, c, raws[q, c])
             gather(q, 0, S)
         HALF = S // 2
-        woven0 = [weave(0, a, a + HALF, True) for a in (0, HALF)]
+        QUARTER = S // 4
+        woven0 = [weave(0, a, a + HALF, True, own_woven(0, a, a + HALF)) for a in (0, HALF)]
         for i, a in enumerate((0, HALF)):
             quantize(0, a, a + HALF, woven0[i])
-        w_woven = []
-        for g in range(PASSES):
-            held = keep.tile([P, N, PACK], BF16, name="w_woven_%d" % g, align_bytes=64)
-            nc.vector.tensor_copy(out=held[:], in_=w_raw[g][:].rearrange("p j m -> p m j"))
-            w_woven.append(held)
-        for g in range(PASSES):
-            nc.vector.quantize_mx(
-                out=w_codes[g][:].bitcast(FP8X4), scales=w_scales[g][:], in_=w_woven[g][:].rearrange("p m j -> p (m j)")
-            )
-        QUARTER = S // 4
-        acc0 = [bank(QUARTER) for i in range(4)]
-        acc1 = [bank_b(HALF) for i in range(2)]
-        for i in range(4):
-            multiply(acc0[i], 0, 0, i * QUARTER, (i + 1) * QUARTER)
-        for i in range(2):
-            multiply(acc1[i], 1, 0, i * HALF, (i + 1) * HALF)
 
         for c in range(len(CHUNKS[2])):
             cast_chunk(2, c, raws[2, c])
@@ -182,17 +191,32 @@ def tile_picked_bilin_none_e_kernel(tc, xT, w1, fx, fy, offs, c00, c01, c10, c11
         for c in range(len(CHUNKS[3])):
             cast_chunk(3, c, raws[3, c])
         y = [keep.tile([P, S], F32, name="y_%d" % blk) for blk in range(2)]
+        cuts = ((0, 256), (256, 512), (512, 768), (768, 896), (896, 1024))
+        acc0 = [bank(b - a) for a, b in cuts[:3]] + [bank_b(b - a) for a, b in cuts[3:]]
+        w_woven0 = [
+            weave_w(0, g, picked[1][:, S + (2 + g) * QUARTER : S + (3 + g) * QUARTER].bitcast(BF16)) for g in range(PASSES)
+        ]
+        for g in range(PASSES):
+            quantize_w(0, g, w_woven0[g])
+        for j, (c, d) in enumerate(cuts):
+            multiply(acc0[j], 0, 0, c, d)
         woven1 = []
-        for i in range(4):
-            gather(3, i * QUARTER, (i + 1) * QUARTER)
-            woven1.append(weave(1, i * QUARTER, (i + 1) * QUARTER, False))
-        for i in range(4):
-            quantize(1, i * QUARTER, (i + 1) * QUARTER, woven1[i])
-            multiply(acc0[i], 0, 1, i * QUARTER, (i + 1) * QUARTER)
-            nc.scalar.copy(out=y[0][:, i * QUARTER : (i + 1) * QUARTER], in_=acc0[i][:])
+        for a, b in cuts:
+            if a % QUARTER == 0:
+                gather(3, a, a + QUARTER)
+            woven1.append(weave(1, a, b, False, own_woven(1, a, b)))
+        for i, (a, b) in enumerate(cuts):
+            quantize(1, a, b, woven1[i])
+            multiply(acc0[i], 0, 1, a, b)
+            nc.scalar.copy(out=y[0][:, a:b], in_=acc0[i][:])
+        late = [weave_w(1, g, own_w(1, g, tag)) for g, tag in enumerate(("woven_1_256", "woven_1_896"))]
+        for g in range(PASSES):
+            quantize_w(1, g, late[g])
         for i in range(2):
-            multiply(acc1[i], 1, 1, i * HALF, (i + 1) * HALF)
-            nc.scalar.copy(out=y[1][:, i * HALF : (i + 1) * HALF], in_=acc1[i][:])
+            acc1 = bank_b(HALF)
+            for g in range(PASSES):
+                multiply(acc1, 1, g, i * HALF, (i + 1) * HALF)
+            nc.scalar.copy(out=y[1][:, i * HALF : (i + 1) * HALF], in_=acc1[:])
 
         def weighted(blk, corner, a, b):
             prod = keep.tile([P, b - a], F32, name="prod_%d_%d_%d" % (blk, corner, a))
@@ -221,16 +245,16 @@ def tile_picked_bilin_none_e_kernel(tc, xT, w1, fx, fy, offs, c00, c01, c10, c11
         nc.scalar.copy(out=result[:], in_=back[:])
         nc.sync.dma_start(out=out[0:P, :], in_=result[:])
 
-        HV = V // 2
+        pieces = ((0, V - P), (V - P, V))
         sums = [bank(P) for s in range(V // P)]
         for corner in range(2):
             add_turned(sums, weighted(1, corner, 0, V), 0, V, corner == 0, False)
         backs = []
-        for a in (0, HV):
-            add_turned(sums, weighted(1, 2, a, a + HV), a, a + HV, False, True)
-            backs.append(turn_back(1, sums, a, a + HV))
-        lasts = [weighted(1, 3, a, a + HV) for a in (0, HV)]
-        for i, a in enumerate((0, HV)):
-            result = keep.tile([P, HV], F32, name="result_1_%d" % i)
-            nc.vector.tensor_tensor(result[:], backs[i][:], lasts[i][:], ADD)
-            nc.sync.dma_start(out=out[P : 2 * P, a : a + HV], in_=result[:])
+        for a, b in pieces:
+            add_turned(sums, weighted(1, 2, a, b), a, b, False, True)
+            backs.append(turn_back(1, sums, a, b))
+        last = weighted(1, 3, 0, V)
+        for i, (a, b) in enumerate(pieces):
+            result = keep.tile([P, b - a], F32, name="result_1_%d" % i)
+            nc.vector.tensor_tensor(result[:], backs[i][:], last[:, a:b], ADD)
+            nc.sync.dma_start(out=out[P : 2 * P, a:b], in_=result[:])

@@ -23,8 +23,8 @@ PASSES = K // K_PASS
 LANES = 16
 
 CHUNKS = [
-    [(1280, 2048, 0), (640, 1280, 0), (0, 640, 0)],
-    [(1024, 2048, 0), (0, 1024, 640)],
+    [(1024, 2048, 1024), (0, 1024, 1024)],
+    [(1024, 2048, 0), (0, 1024, 688)],
     [(1280, 2048, 0), (640, 1280, 0), (0, 640, 0)],
     [(1024, 2048, 0), (512, 1024, 512), (0, 512, 336)],
 ]
@@ -114,14 +114,13 @@ def tile_picked_bilin_none_e_kernel(tc, xT, w1, fx, fy, offs, c00, c01, c10, c11
             )
 
         raws = {}
+        raws[0, 0] = load_chunk(0, 0)
         fx_sb = keep.tile([P, PACK], F32, name="fx_sb")
         fy_sb = keep.tile([P, PACK], F32, name="fy_sb")
         nc.sync.dma_start(out=fx_sb[:], in_=fx[0:1, :].rearrange("o (p c) -> (o p) c", c=PACK))
         nc.sync.dma_start(out=fy_sb[:], in_=fy[0:1, :].rearrange("o (p c) -> (o p) c", c=PACK))
-        raws[0, 0] = load_chunk(0, 0)
         raws[0, 1] = load_chunk(0, 1)
         offs_sb = load_list(offs, "offs_sb")
-        raws[0, 2] = load_chunk(0, 2)
         for c in range(len(CHUNKS[1])):
             raws[1, c] = load_chunk(1, c)
         for q in (2, 3):
@@ -170,7 +169,7 @@ def tile_picked_bilin_none_e_kernel(tc, xT, w1, fx, fy, offs, c00, c01, c10, c11
             for c in range(PACK):
                 nc.tensor.transpose(spread[:, c * P : (c + 1) * P], small[:, c : c + 1].to_broadcast([P, P]), ident[:])
             wide = keep.tile([P, V], F32, name="wide_%d" % corner)
-            nc.vector.tensor_copy(
+            nc.scalar.copy(
                 out=wide[:].rearrange("p (n c) -> p n c", c=PACK), in_=spread[:].rearrange("p (c n) -> p n c", c=PACK)
             )
             weights.append(wide)
@@ -193,11 +192,7 @@ def tile_picked_bilin_none_e_kernel(tc, xT, w1, fx, fy, offs, c00, c01, c10, c11
         y = [keep.tile([P, S], F32, name="y_%d" % blk) for blk in range(2)]
         cuts = ((0, 256), (256, 512), (512, 768), (768, 896), (896, 1024))
         acc0 = [bank(b - a) for a, b in cuts[:3]] + [bank_b(b - a) for a, b in cuts[3:]]
-        w_woven0 = [
-            weave_w(0, g, picked[1][:, S + (2 + g) * QUARTER : S + (3 + g) * QUARTER].bitcast(BF16)) for g in range(PASSES)
-        ]
-        for g in range(PASSES):
-            quantize_w(0, g, w_woven0[g])
+        quantize_w(0, 0, weave_w(0, 0, picked[1][:, S + 2 * QUARTER : S + 3 * QUARTER].bitcast(BF16)))
         for j, (c, d) in enumerate(cuts):
             multiply(acc0[j], 0, 0, c, d)
         woven1 = []
@@ -205,11 +200,15 @@ def tile_picked_bilin_none_e_kernel(tc, xT, w1, fx, fy, offs, c00, c01, c10, c11
             if a % QUARTER == 0:
                 gather(3, a, a + QUARTER)
             woven1.append(weave(1, a, b, False, own_woven(1, a, b)))
+            if a == 0:
+                held = weave_w(0, 1, own_w(0, 1, "w_woven_0_1"))
         for i, (a, b) in enumerate(cuts):
             quantize(1, a, b, woven1[i])
+            if i == 0:
+                quantize_w(0, 1, held)
             multiply(acc0[i], 0, 1, a, b)
             nc.scalar.copy(out=y[0][:, a:b], in_=acc0[i][:])
-        late = [weave_w(1, g, own_w(1, g, tag)) for g, tag in enumerate(("woven_1_256", "woven_1_896"))]
+        late = [weave_w(1, g, own_w(1, g, tag)) for g, tag in enumerate(("woven_1_768", "woven_1_896"))]
         for g in range(PASSES):
             quantize_w(1, g, late[g])
         for i in range(2):
@@ -257,4 +256,5 @@ def tile_picked_bilin_none_e_kernel(tc, xT, w1, fx, fy, offs, c00, c01, c10, c11
         for i, (a, b) in enumerate(pieces):
             result = keep.tile([P, b - a], F32, name="result_1_%d" % i)
             nc.vector.tensor_tensor(result[:], backs[i][:], last[:, a:b], ADD)
-            nc.sync.dma_start(out=out[P : 2 * P, a:b], in_=result[:])
+            queue = nc.sync if i == 0 else nc.scalar
+            queue.dma_start(out=out[P : 2 * P, a:b], in_=result[:])

from contextlib import ExitStack

import concourse.mybir as mybir
from concourse.masks import make_identity

K, T, S, V, N = 1024, 2048, 1024, 512, 256
FLOPS = 2 * K * S * N

F32 = mybir.dt.float32
BF16 = mybir.dt.bfloat16
U32 = mybir.dt.uint32
I32 = mybir.dt.int32
U16 = mybir.dt.uint16
U8 = mybir.dt.uint8
FP8X4 = mybir.dt.float8_e4m3fn_x4
MULT = mybir.AluOpType.mult
ADD = mybir.AluOpType.add

P = 128
PACK = 4
K_PASS = P * PACK
PASSES = K // K_PASS
LANES = 16

CHUNKS = [
    [(1024, 2048, 1024), (0, 1024, 1024)],
    [(1024, 2048, 0), (0, 1024, 688)],
    [(1280, 2048, 0), (640, 1280, 0), (0, 640, 0)],
    [(1024, 2048, 0), (512, 1024, 512), (0, 512, 336)],
]


def tile_picked_bilin_none_e_kernel(tc, xT, w1, fx, fy, offs, c00, c01, c10, c11, out):
    nc = tc.nc
    with ExitStack() as ctx:
        keep = ctx.enter_context(tc.tile_pool(name="keep", bufs=1))
        psum = ctx.enter_context(tc.psum_pool(name="psum", bufs=4))
        psum_b = ctx.enter_context(tc.psum_pool(name="psum_b", bufs=2))

        def bank(width):
            return psum.tile([P, width], F32, name="bank")

        def bank_b(width):
            return psum_b.tile([P, width], F32, name="bank_b")

        def load_list(src, name):
            held = keep.tile([P, src.shape[1]], U16, name=name)
            nc.sync.dma_start(held[:], src)
            return held

        def entries(held, a, b):
            return held[:, a // LANES : b // LANES]

        def load_chunk(q, c):
            g, u = divmod(q, 2)
            a, b = CHUNKS[q][c][:2]
            raw = keep.tile([P, 2, b - a], F32, name="raw_%d_%d" % (q, c), align_bytes=64)
            rows = xT[g * K_PASS : (g + 1) * K_PASS, a:b].rearrange("(p j) t -> p j t", j=PACK)
            nc.sync.dma_start(out=raw[:], in_=rows[:, 2 * u : 2 * u + 2, :])
            return raw

        pair_tiles = [keep.tile([P, T], U32, name="pairs_%d" % q) for q in range(2 * PASSES)]
        pairs = [held[:] for held in pair_tiles]

        def cast_chunk(q, c, raw):
            a, b, on_vector = CHUNKS[q][c]
            dst = pairs[q].bitcast(BF16).rearrange("p (t e) -> p t e", e=2)
            src = raw[:].rearrange("p e t -> p t e")
            if on_vector < b - a:
                nc.scalar.copy(out=dst[:, a + on_vector : b, :], in_=src[:, on_vector:, :])
            if on_vector:
                nc.vector.tensor_copy(out=dst[:, a : a + on_vector, :], in_=src[:, :on_vector, :])

        picked = [keep.tile([P, 2 * S], U32, name="picked_%d" % g, align_bytes=64) for g in range(PASSES)]
        x_codes = [keep.tile([P, S], U32, name="x_codes_%d" % g, align_bytes=64) for g in range(PASSES)]
        x_scales = [keep.tile([P, S], U8, name="x_scales_%d" % g, align_bytes=64) for g in range(PASSES)]
        w_codes = [keep.tile([P, PASSES * P], U32, name="w_codes_%d" % blk, align_bytes=64) for blk in range(2)]
        w_scales = [keep.tile([P, PASSES * P], U8, name="w_scales_%d" % blk, align_bytes=64) for blk in range(2)]

        def gather(q, a, b):
            g, u = divmod(q, 2)
            nc.vector.tensor_copy(picked[g][:, u * S + a : u * S + b], pairs[q].indirect(entries(offs_sb, a, b)))

        def own_woven(g, a, b):
            woven = keep.tile([P, 2 * (b - a)], U32, name="woven_%d_%d" % (g, a), align_bytes=64)
            return woven[:]

        def weave(g, a, b, on_vector, woven):
            src = picked[g][:].rearrange("p (u t) -> p u t", u=2)[:, :, a:b]
            if on_vector:
                nc.vector.tensor_copy(
                    out=woven.bitcast(I32).rearrange("p (t u) -> p t u", u=2),
                    in_=src.bitcast(I32).rearrange("p u t -> p t u"),
                )
            else:
                nc.scalar.copy(out=woven.rearrange("p (t u) -> p t u", u=2), in_=src.rearrange("p u t -> p t u"))
            return woven

        def quantize(g, a, b, woven):
            nc.vector.quantize_mx(
                out=x_codes[g][:, a:b].bitcast(FP8X4), scales=x_scales[g][:, a:b], in_=woven.bitcast(BF16)
            )

        def multiply(acc, blk, g, a, b):
            rows = slice(g * P, (g + 1) * P)
            nc.tensor.matmul_mx(
                out=acc[:],
                lhsT=w_codes[blk][:, rows].bitcast(FP8X4),
                lhsT_scale=w_scales[blk][:, rows],
                rhs=x_codes[g][:, a:b].bitcast(FP8X4),
                rhs_scale=x_scales[g][:, a:b],
                start=(g == 0),
                stop=(g == PASSES - 1),
            )

        raws = {}
        raws[0, 0] = load_chunk(0, 0)
        fx_sb = keep.tile([P, PACK], F32, name="fx_sb")
        fy_sb = keep.tile([P, PACK], F32, name="fy_sb")
        nc.sync.dma_start(out=fx_sb[:], in_=fx[0:1, :].rearrange("o (p c) -> (o p) c", c=PACK))
        nc.sync.dma_start(out=fy_sb[:], in_=fy[0:1, :].rearrange("o (p c) -> (o p) c", c=PACK))
        raws[0, 1] = load_chunk(0, 1)
        offs_sb = load_list(offs, "offs_sb")
        for c in range(len(CHUNKS[1])):
            raws[1, c] = load_chunk(1, c)
        for q in (2, 3):
            for c in range(len(CHUNKS[q])):
                raws[q, c] = load_chunk(q, c)

        def load_w(blk, g):
            held = keep.tile([P, PACK, P], F32, name="w_raw_%d_%d" % (blk, g), align_bytes=64)
            rows = w1[g * K_PASS : (g + 1) * K_PASS, blk * P : (blk + 1) * P]
            nc.sync.dma_start(out=held[:], in_=rows.rearrange("(p j) m -> p j m", j=PACK))
            return held

        w_raw = {(0, g): load_w(0, g) for g in range(PASSES)}
        corners = [load_list(src, name) for src, name in ((c00, "c00_sb"), (c01, "c01_sb"), (c10, "c10_sb"), (c11, "c11_sb"))]
        for g in range(PASSES):
            w_raw[1, g] = load_w(1, g)

        def own_w(blk, g, tag):
            held = keep.tile([P, P * PACK], BF16, name="w_woven_%d_%d" % (blk, g), tag=tag, align_bytes=64)
            return held[:]

        def weave_w(blk, g, held):
            dst = held.rearrange("p (m j) -> p m j", j=PACK)
            src = w_raw[blk, g][:].rearrange("p j m -> p m j")
            if blk == 0:
                nc.scalar.copy(out=dst, in_=src)
            else:
                nc.vector.tensor_copy(out=dst, in_=src)
            return held

        def quantize_w(blk, g, held):
            rows = slice(g * P, (g + 1) * P)
            nc.vector.quantize_mx(out=w_codes[blk][:, rows].bitcast(FP8X4), scales=w_scales[blk][:, rows], in_=held)

        ident = keep.tile([P, P], F32, name="ident")
        make_identity(nc, ident[:])
        gx = keep.tile([P, PACK], F32, name="gx")
        gy = keep.tile([P, PACK], F32, name="gy")
        nc.vector.tensor_scalar(gx[:], fx_sb[:], -1.0, 1.0, MULT, ADD)
        nc.vector.tensor_scalar(gy[:], fy_sb[:], -1.0, 1.0, MULT, ADD)
        weights = []
        for corner, (along_x, along_y) in enumerate(((gx, gy), (fx_sb, gy), (gx, fy_sb), (fx_sb, fy_sb))):
            small = keep.tile([P, PACK], F32, name="small_%d" % corner)
            nc.vector.tensor_tensor(small[:], along_x[:], along_y[:], MULT)
            spread = bank(V)
            for c in range(PACK):
                nc.tensor.transpose(spread[:, c * P : (c + 1) * P], small[:, c : c + 1].to_broadcast([P, P]), ident[:])
            wide = keep.tile([P, V], F32, name="wide_%d" % corner)
            nc.scalar.copy(
                out=wide[:].rearrange("p (n c) -> p n c", c=PACK), in_=spread[:].rearrange("p (c n) -> p n c", c=PACK)
            )
            weights.append(wide)

        for q in (0, 1):
            for c in range(len(CHUNKS[q])):
                cast_chunk(q, c, raws[q, c])
            gather(q, 0, S)
        HALF = S // 2
        QUARTER = S // 4
        woven0 = [weave(0, a, a + HALF, True, own_woven(0, a, a + HALF)) for a in (0, HALF)]
        for i, a in enumerate((0, HALF)):
            quantize(0, a, a + HALF, woven0[i])

        for c in range(len(CHUNKS[2])):
            cast_chunk(2, c, raws[2, c])
        gather(2, 0, S)
        for c in range(len(CHUNKS[3])):
            cast_chunk(3, c, raws[3, c])
        y = [keep.tile([P, S], F32, name="y_%d" % blk) for blk in range(2)]
        cuts = ((0, 256), (256, 512), (512, 768), (768, 896), (896, 1024))
        acc0 = [bank(b - a) for a, b in cuts[:3]] + [bank_b(b - a) for a, b in cuts[3:]]
        quantize_w(0, 0, weave_w(0, 0, picked[1][:, S + 2 * QUARTER : S + 3 * QUARTER].bitcast(BF16)))
        for j, (c, d) in enumerate(cuts):
            multiply(acc0[j], 0, 0, c, d)
        woven1 = []
        for a, b in cuts:
            if a % QUARTER == 0:
                gather(3, a, a + QUARTER)
            woven1.append(weave(1, a, b, False, own_woven(1, a, b)))
            if a == 0:
                held = weave_w(0, 1, own_w(0, 1, "w_woven_0_1"))
        for i, (a, b) in enumerate(cuts):
            quantize(1, a, b, woven1[i])
            if i == 0:
                quantize_w(0, 1, held)
            multiply(acc0[i], 0, 1, a, b)
            nc.scalar.copy(out=y[0][:, a:b], in_=acc0[i][:])
        late = [weave_w(1, g, own_w(1, g, tag)) for g, tag in enumerate(("woven_1_768", "woven_1_896"))]
        for g in range(PASSES):
            quantize_w(1, g, late[g])
        for i in range(2):
            acc1 = bank_b(HALF)
            for g in range(PASSES):
                multiply(acc1, 1, g, i * HALF, (i + 1) * HALF)
            nc.scalar.copy(out=y[1][:, i * HALF : (i + 1) * HALF], in_=acc1[:])

        def weighted(blk, corner, a, b):
            prod = keep.tile([P, b - a], F32, name="prod_%d_%d_%d" % (blk, corner, a))
            nc.vector.tensor_tensor(prod[:], y[blk][:].indirect(entries(corners[corner], a, b)), weights[corner][:, a:b], MULT)
            return prod

        def add_turned(sums, prod, a, b, first, last):
            for s in range(a // P, b // P):
                nc.tensor.matmul(
                    sums[s][:], prod[:, s * P - a : (s + 1) * P - a], ident[:], start=first, stop=last, is_transpose=True
                )

        def turn_back(blk, sums, a, b):
            back = bank_b(b - a)
            for s in range(a // P, b // P):
                turned = keep.tile([P, P], F32, name="turned_%d_%d" % (blk, s))
                nc.scalar.copy(out=turned[:], in_=sums[s][:])
                nc.tensor.transpose(back[:, s * P - a : (s + 1) * P - a], turned[:], ident[:])
            return back

        sums = [bank(P) for s in range(V // P)]
        for corner in range(4):
            add_turned(sums, weighted(0, corner, 0, V), 0, V, corner == 0, corner == 3)
        back = turn_back(0, sums, 0, V)
        result = keep.tile([P, V], F32, name="result_0")
        nc.scalar.copy(out=result[:], in_=back[:])
        nc.sync.dma_start(out=out[0:P, :], in_=result[:])

        pieces = ((0, V - P), (V - P, V))
        sums = [bank(P) for s in range(V // P)]
        for corner in range(2):
            add_turned(sums, weighted(1, corner, 0, V), 0, V, corner == 0, False)
        backs = []
        for a, b in pieces:
            add_turned(sums, weighted(1, 2, a, b), a, b, False, True)
            backs.append(turn_back(1, sums, a, b))
        last = weighted(1, 3, 0, V)
        for i, (a, b) in enumerate(pieces):
            result = keep.tile([P, b - a], F32, name="result_1_%d" % i)
            nc.vector.tensor_tensor(result[:], backs[i][:], last[:, a:b], ADD)
            queue = nc.sync if i == 0 else nc.scalar
            queue.dma_start(out=out[P : 2 * P, a:b], in_=result[:])
